import numpy as np
import ml_dtypes


def mxq(x, axis, fmt="e4m3"):
    dtype, down = {"e4m3": (ml_dtypes.float8_e4m3fn, 7), "e5m2": (ml_dtypes.float8_e5m2, 14)}[fmt]
    v = np.moveaxis(np.asarray(x, np.float32).astype(ml_dtypes.bfloat16).astype(np.float64), axis, -1)
    blocks = v.reshape(v.shape[:-1] + (-1, 32))
    amax = np.abs(blocks).max(-1, keepdims=True)
    byte = np.maximum(np.where(amax > 0, np.frexp(amax)[1] - 1 + 127, 0) - down, 1)
    scale = np.exp2(byte - 127.0)
    codes = (blocks / scale).astype(np.float32).astype(dtype).astype(np.float64)
    return np.moveaxis((codes * scale).reshape(v.shape), -1, axis)


WIDE = False


def mx_kscale(k):
    if not WIDE:
        return np.ones(k)
    levels = np.array([30, -30])
    if k % 512:
        return np.exp2(np.random.permutation(np.resize(levels, k // 32))).repeat(32)
    a = np.empty((k // 512, 16))
    for p in range(k // 512):
        a[p, :8] = np.random.permutation(np.resize(levels, 8))
        for g in range(8):
            far = levels[np.abs(levels - a[p, g]) >= 10]
            a[p, g + 8] = far[np.random.randint(len(far))]
    return np.exp2(a.ravel()).repeat(32)


def f64(x):
    return np.asarray(x).astype(np.float64)


def striped(idx):
    return np.tile(np.asarray(idx).reshape(-1, 16).T, (8, 1)).astype(np.uint16)


def unstriped(offs):
    return offs[:16].T.reshape(-1).astype(np.int64)


def bf(x):
    return np.asarray(x, np.float32).astype(ml_dtypes.bfloat16)


def planes(Y):
    r, m = Y.shape
    b = f64(bf(Y)).reshape(r // 32, 32, m)
    amax = np.abs(b).max(1)
    byte = np.clip(np.where(amax > 0, np.frexp(amax)[1] - 1 + 127 - 7, 1), 1, 254)
    codes = (b * np.exp2(127.0 - byte)[:, None, :]).reshape(r, m).astype(np.float32).astype(ml_dtypes.float8_e4m3fn).view(np.uint8)
    words = codes.reshape(r // 512, 128, 4, m).transpose(0, 1, 3, 2)
    return np.ascontiguousarray(words), np.ascontiguousarray(byte.astype(np.uint8).reshape(r // 512, 16, m))


K, J, N, T, V, C = 512, 512, 256, 1024, 1024, 64


def setup_inputs():
    n = np.random.standard_normal
    idx = np.random.permutation(T)[:J]
    idx2 = np.random.permutation(T)[:J]
    idx3 = np.random.permutation(V)[:J]
    fj = mx_kscale(J)
    return {
        "xf": (n((K, T))).astype(np.float32),
        "ra": (np.random.uniform(0.5, 1.5, (1, J)) * fj).astype(np.float32),
        "gt": (n((N, V)) * np.exp(0.5 * n((1, V)))).astype(np.float32),
        "rb": (np.random.uniform(0.5, 1.5, (1, J)) / fj).astype(np.float32),
        "pc1": (np.random.uniform(0.02, 0.08, (K, N))).astype(np.float32),
        "old": (0.5 * n((K, N))).astype(np.float32),
        "offs": striped(idx),
        "offs2": striped(idx2),
        "offs3": striped(idx3),
    }


def reference(xf, ra, gt, rb, pc1, old, offs, offs2, offs3):
    idx = unstriped(offs)
    idx2 = unstriped(offs2)
    idx3 = unstriped(offs3)
    us = np.maximum(f64(xf)[:, idx], f64(xf)[:, idx2]) * f64(ra)
    uj = us.T
    gg = f64(gt)[:, idx3]
    c1 = gg.reshape(N, C, J // C).mean(axis=2)
    c2 = np.repeat(c1, J // C, axis=1)
    gs = (gg - c2) * f64(rb)
    gj = gs.T
    ujq = mxq(uj, 0, "e5m2")
    gjq = mxq(gj, 0, "e5m2")
    w = ujq.T @ gjq
    w2 = w * f64(pc1)
    y = f64(old) - w2 + 0.2 * np.mean(w2, axis=1, keepdims=True)
    words, scales = planes(y)
    return y, words, scales

@@ -1,0 +1,211 @@
+from contextlib import ExitStack
+
+import concourse.mybir as mybir
+from concourse.masks import make_identity
+
+K, J, N, T, V, C = 512, 512, 256, 1024, 1024, 64
+FLOPS = 2 * K * J * N
+
+F32 = mybir.dt.float32
+BF16 = mybir.dt.bfloat16
+I32 = mybir.dt.int32
+U32 = mybir.dt.uint32
+U16 = mybir.dt.uint16
+U8 = mybir.dt.uint8
+E5M2X4 = mybir.dt.float8_e5m2_x4
+E4M3X4 = mybir.dt.float8_e4m3fn_x4
+ALU = mybir.AluOpType
+COPY = mybir.ActivationFunctionType.Copy
+
+P = 128
+PACK = 4
+SET = J // C
+CAST_SPLIT = 176
+
+
+def tile_list_moment_larger_centred_preconditioned_pl_kernel(
+    tc, xf, ra, gt, rb, pc1, old, offs, offs2, offs3, out_0, out_1, out_2
+):
+    nc = tc.nc
+    with ExitStack() as ctx:
+        keep = ctx.enter_context(tc.tile_pool(name="keep", bufs=1))
+        turn = ctx.enter_context(tc.psum_pool(name="turn", bufs=4))
+        sums = ctx.enter_context(tc.psum_pool(name="sums", bufs=4))
+
+        list1 = keep.tile([P, J // 16], U16, name="list1")
+        list2 = keep.tile([P, J // 16], U16, name="list2")
+        list3 = keep.tile([P, J // 16], U16, name="list3")
+        x_win = [keep.tile([P, T], F32, name="x_win%d" % t) for t in range(PACK)]
+        g_win = [keep.tile([P, V], F32, name="g_win%d" % h) for h in range(2)]
+        ra_sb = keep.tile([P, PACK], F32, name="ra_sb")
+        rb_sb = keep.tile([P, PACK], F32, name="rb_sb")
+        pc_sb = keep.tile([P, PACK, N], F32, name="pc_sb")
+        old_sb = keep.tile([P, PACK, N], F32, name="old_sb")
+        ident = keep.tile([P, P], F32, name="ident")
+
+        xf_rows = xf.rearrange("(p t) c -> p t c", t=PACK)
+        nc.sync.dma_start(x_win[0][:], xf_rows[:, 0, :])
+        nc.sync.dma_start(list1[:], offs)
+        nc.sync.dma_start(list2[:], offs2)
+        nc.sync.dma_start(x_win[1][:], xf_rows[:, 1, :])
+        nc.sync.dma_start(list3[:], offs3)
+        nc.sync.dma_start(g_win[0][:], gt[0:P, :])
+        nc.sync.dma_start(ra_sb[:], ra.rearrange("o (p s) -> p (o s)", s=PACK))
+        nc.sync.dma_start(rb_sb[:], rb.rearrange("o (p s) -> p (o s)", s=PACK))
+        nc.sync.dma_start(g_win[1][:], gt[P : 2 * P, :])
+        for t in range(2, PACK):
+            nc.sync.dma_start(x_win[t][:], xf_rows[:, t, :])
+        nc.sync.dma_start(pc_sb[:], pc1.rearrange("(p t) n -> p t n", t=PACK))
+        nc.sync.dma_start(old_sb[:], old.rearrange("(p t) n -> p t n", t=PACK))
+        make_identity(nc, ident[:])
+
+        def gather(engine, name, window, offsets):
+            picked = keep.tile([P, J], F32, name=name)
+            if engine == "vector":
+                nc.vector.tensor_copy(picked[:], window[:].indirect(offsets[:]))
+            else:
+                nc.scalar.activation(picked[:], window[:].indirect(offsets[:]), COPY)
+            return picked
+
+        def weigh_and_round(rounded, bank, weight):
+            nc.vector.tensor_tensor(
+                rounded,
+                bank[:].rearrange("q s c -> q c s"),
+                weight[:].unsqueeze(1).to_broadcast([P, P, PACK]),
+                ALU.mult,
+            )
+
+        g_codes = keep.tile([P, N], U32, name="g_codes", align_bytes=64)
+        g_scales = keep.tile([P, N], U8, name="g_scales", align_bytes=64)
+        u_codes = [keep.tile([P, P], U32, name="u_codes%d" % t, align_bytes=64) for t in range(PACK)]
+        u_scales = [keep.tile([P, P], U8, name="u_scales%d" % t, align_bytes=64) for t in range(PACK)]
+        w2 = keep.tile([P, PACK, N], F32, name="w2")
+        y = keep.tile([P, PACK, N], F32, name="y")
+        row_sum = [keep.tile([P, 1], F32, name="row_sum%d" % t) for t in range(PACK)]
+        shift = [keep.tile([P, 1], F32, name="shift%d" % t) for t in range(PACK)]
+        out_rows = out_0.rearrange("(p t) n -> p t n", t=PACK)
+
+        def u_turn(t, first, second):
+            larger = keep.tile([P, PACK, P], F32, name="larger%d" % t)
+            nc.vector.tensor_tensor(
+                larger[:].rearrange("p s q -> p q s"),
+                first[:].rearrange("p (q s) -> p q s", s=PACK),
+                second[:].rearrange("p (q s) -> p q s", s=PACK),
+                ALU.max,
+            )
+            bank = turn.tile([P, PACK, P], F32, name="bank")
+            for s in range(PACK):
+                nc.tensor.transpose(bank[:, s, :], larger[:, s, :], ident[:])
+            return bank
+
+        def u_quantise(t, rounded):
+            nc.vector.quantize_mx(
+                out=u_codes[t][:].bitcast(E5M2X4),
+                scales=u_scales[t][:],
+                in_=rounded.rearrange("q c s -> q (c s)"),
+            )
+
+        def g_turn(h, picked):
+            set_sum = keep.tile([P, C], F32, name="set_sum%d" % h)
+            nc.vector.tensor_reduce(
+                set_sum[:], picked[:].rearrange("p (c i) -> p c i", i=SET), mybir.AxisListType.X, ALU.add
+            )
+            neg_mean = keep.tile([P, C, 2], F32, name="neg_mean%d" % h)
+            nc.vector.tensor_scalar(
+                neg_mean[:], set_sum[:].unsqueeze(2).to_broadcast([P, C, 2]), -1.0 / SET, None, ALU.mult
+            )
+            bank = turn.tile([P, PACK, P], F32, name="bank")
+            for s in range(PACK):
+                nc.tensor.matmul(
+                    bank[:, s, :], picked[:, s:J:PACK], ident[:], start=(s == 0), stop=False, is_transpose=True
+                )
+            for s in range(PACK):
+                nc.tensor.matmul(
+                    bank[:, s, :],
+                    neg_mean[:].rearrange("p c e -> p (c e)"),
+                    ident[:],
+                    start=False,
+                    stop=(s == PACK - 1),
+                    is_transpose=True,
+                )
+            return bank
+
+        def weigh(t):
+            acc = sums.tile([P, N], F32, name="acc")
+            nc.tensor.matmul_mx(
+                out=acc[:],
+                lhsT=u_codes[t][:].bitcast(E5M2X4),
+                lhsT_scale=u_scales[t][:],
+                rhs=g_codes[:].bitcast(E5M2X4),
+                rhs_scale=g_scales[:],
+                start=True,
+                stop=True,
+            )
+            nc.vector.scalar_tensor_tensor(
+                w2[:, t, :], acc[:], 1.0, pc_sb[:, t, :], ALU.mult, ALU.mult, accum_out=row_sum[t][:]
+            )
+            nc.scalar.activation(shift[t][:], row_sum[t][:], COPY, scale=0.2 / N)
+
+        def update(t):
+            nc.vector.scalar_tensor_tensor(
+                y[:, t, :], old_sb[:, t, :], shift[t][:], w2[:, t, :], ALU.add, ALU.subtract
+            )
+            nc.sync.dma_start(out_rows[:, t, :], y[:, t, :])
+
+        u_bf = [keep.tile([P, P, PACK], BF16, name="u_bf%d" % t, align_bytes=64) for t in range(PACK)]
+        g_bf = keep.tile([P, N, PACK], BF16, name="g_bf", align_bytes=64)
+
+        a0 = gather("vector", "a0", x_win[0], list1)
+        b0 = gather("scalar", "b0", x_win[0], list2)
+        u0 = u_turn(0, a0, b0)
+        a1 = gather("vector", "a1", x_win[1], list1)
+        b1 = gather("scalar", "b1", x_win[1], list2)
+        u1 = u_turn(1, a1, b1)
+        g0 = gather("scalar", "g0", g_win[0], list3)
+        g1 = gather("scalar", "g1", g_win[1], list3)
+        a2 = gather("scalar", "a2", x_win[2], list1)
+        b2 = gather("scalar", "b2", x_win[2], list2)
+        a3 = gather("scalar", "a3", x_win[3], list1)
+        b3 = gather("scalar", "b3", x_win[3], list2)
+        weigh_and_round(u_bf[0][:], u0, ra_sb)
+        v0 = g_turn(0, g0)
+        weigh_and_round(u_bf[1][:], u1, ra_sb)
+        v1 = g_turn(1, g1)
+        u_quantise(0, u_bf[0][:])
+        u_quantise(1, u_bf[1][:])
+        weigh_and_round(g_bf[:, 0:P, :], v0, rb_sb)
+        u2 = u_turn(2, a2, b2)
+        weigh_and_round(g_bf[:, P:N, :], v1, rb_sb)
+        weigh_and_round(u_bf[2][:], u2, ra_sb)
+        nc.vector.quantize_mx(
+            out=g_codes[:].bitcast(E5M2X4), scales=g_scales[:], in_=g_bf[:].rearrange("q c s -> q (c s)")
+        )
+        u_quantise(2, u_bf[2][:])
+        u3 = u_turn(3, a3, b3)
+        weigh(0)
+        weigh(1)
+        weigh_and_round(u_bf[3][:], u3, ra_sb)
+        update(0)
+        u_quantise(3, u_bf[3][:])
+        weigh(2)
+        update(1)
+        weigh(3)
+        update(2)
+        update(3)
+
+        y_bf = keep.tile([P, N, PACK], BF16, name="y_bf", align_bytes=64)
+        y_woven = y[:].rearrange("p t n -> p n t")
+        nc.vector.tensor_copy(y_bf[:, :CAST_SPLIT, :], y_woven[:, :CAST_SPLIT, :])
+        nc.scalar.copy(y_bf[:, CAST_SPLIT:, :], y_woven[:, CAST_SPLIT:, :])
+        y_codes = keep.tile([P, N], U32, name="y_codes", align_bytes=64)
+        y_scales = keep.tile([P, N], U8, name="y_scales", align_bytes=64)
+        nc.vector.quantize_mx(
+            out=y_codes[:].bitcast(E4M3X4), scales=y_scales[:], in_=y_bf[:].rearrange("p n t -> p (n t)")
+        )
+        nc.sync.dma_start(out_1[0].rearrange("p c r -> p (c r)").bitcast(I32), y_codes[:].bitcast(I32))
+        for quad in range(4):
+            queue = nc.scalar if quad % 2 == 0 else nc.sync
+            queue.dma_start(
+                out_2[0, 4 * quad : 4 * quad + 4, :].bitcast(I32),
+                y_scales[32 * quad : 32 * quad + 4, :].bitcast(I32),
+            )

@@ -16,6 +16,7 @@ E5M2X4 = mybir.dt.float8_e5m2_x4
 E4M3X4 = mybir.dt.float8_e4m3fn_x4
 ALU = mybir.AluOpType
 COPY = mybir.ActivationFunctionType.Copy
+IDENTITY = mybir.ActivationFunctionType.Identity
 
 P = 128
 PACK = 4
@@ -45,74 +46,90 @@ def tile_list_moment_larger_centred_preconditioned_pl_kernel(
 
         xf_rows = xf.rearrange("(p t) c -> p t c", t=PACK)
         nc.sync.dma_start(x_win[0][:], xf_rows[:, 0, :])
-        nc.sync.dma_start(list1[:], offs)
         nc.sync.dma_start(list2[:], offs2)
-        nc.sync.dma_start(x_win[1][:], xf_rows[:, 1, :])
+        nc.sync.dma_start(list1[:], offs)
         nc.sync.dma_start(list3[:], offs3)
         nc.sync.dma_start(g_win[0][:], gt[0:P, :])
-        nc.sync.dma_start(ra_sb[:], ra.rearrange("o (p s) -> p (o s)", s=PACK))
-        nc.sync.dma_start(rb_sb[:], rb.rearrange("o (p s) -> p (o s)", s=PACK))
         nc.sync.dma_start(g_win[1][:], gt[P : 2 * P, :])
-        for t in range(2, PACK):
-            nc.sync.dma_start(x_win[t][:], xf_rows[:, t, :])
+        nc.sync.dma_start(ra_sb[:], ra.rearrange("o (p s) -> p (o s)", s=PACK))
+        nc.sync.dma_start(x_win[1][:], xf_rows[:, 1, :])
+        nc.sync.dma_start(rb_sb[:], rb.rearrange("o (p s) -> p (o s)", s=PACK))
+        nc.sync.dma_start(x_win[2][:], xf_rows[:, 2, :])
+        nc.sync.dma_start(x_win[3][:], xf_rows[:, 3, :])
         nc.sync.dma_start(pc_sb[:], pc1.rearrange("(p t) n -> p t n", t=PACK))
         nc.sync.dma_start(old_sb[:], old.rearrange("(p t) n -> p t n", t=PACK))
         make_identity(nc, ident[:])
+        warm_in = keep.tile([P, 1], F32, name="warm_in")
+        warm_out = keep.tile([P, 1], F32, name="warm_out")
+        nc.vector.memset(warm_in[:], 0.0)
+        nc.scalar.activation(warm_out[:], warm_in[:], COPY)
 
-        def gather(engine, name, window, offsets):
-            picked = keep.tile([P, J], F32, name=name)
+        def gather(engine, picked, window, offsets, lo, hi):
+            source = window[:].indirect(offsets[:, lo // 16 : hi // 16])
             if engine == "vector":
-                nc.vector.tensor_copy(picked[:], window[:].indirect(offsets[:]))
+                nc.vector.tensor_copy(picked[:, lo:hi], source)
             else:
-                nc.scalar.activation(picked[:], window[:].indirect(offsets[:]), COPY)
-            return picked
+                nc.scalar.activation(picked[:, lo:hi], source, COPY)
 
-        def weigh_and_round(rounded, bank, weight):
+        def weigh_and_round(target, bank, weight):
             nc.vector.tensor_tensor(
-                rounded,
+                target,
                 bank[:].rearrange("q s c -> q c s"),
                 weight[:].unsqueeze(1).to_broadcast([P, P, PACK]),
                 ALU.mult,
             )
 
-        g_codes = keep.tile([P, N], U32, name="g_codes", align_bytes=64)
-        g_scales = keep.tile([P, N], U8, name="g_scales", align_bytes=64)
-        u_codes = [keep.tile([P, P], U32, name="u_codes%d" % t, align_bytes=64) for t in range(PACK)]
-        u_scales = [keep.tile([P, P], U8, name="u_scales%d" % t, align_bytes=64) for t in range(PACK)]
+        a = [keep.tile([P, J], F32, name="a%d" % t) for t in range(PACK)]
+        b = [keep.tile([P, J], F32, name="b%d" % t) for t in range(PACK)]
+        g = [keep.tile([P, J], F32, name="g%d" % h) for h in range(2)]
+        codes = keep.tile([P, N + K], U32, name="codes", align_bytes=64)
+        scales = keep.tile([P, N + K], U8, name="scales", align_bytes=64)
+        rounded = keep.tile([P, N + K, PACK], BF16, name="rounded", align_bytes=64)
         w2 = keep.tile([P, PACK, N], F32, name="w2")
         y = keep.tile([P, PACK, N], F32, name="y")
-        row_sum = [keep.tile([P, 1], F32, name="row_sum%d" % t) for t in range(PACK)]
+        moved = keep.tile([P, PACK, N], F32, name="moved")
         shift = [keep.tile([P, 1], F32, name="shift%d" % t) for t in range(PACK)]
         out_rows = out_0.rearrange("(p t) n -> p t n", t=PACK)
 
-        def u_turn(t, first, second):
-            larger = keep.tile([P, PACK, P], F32, name="larger%d" % t)
+        def larger_tile(t, tag):
+            return keep.tile([P, PACK, P], F32, name="larger%d" % t, tag=tag, align_bytes=64)
+
+        def take_larger(t, larger, lo, hi):
             nc.vector.tensor_tensor(
-                larger[:].rearrange("p s q -> p q s"),
-                first[:].rearrange("p (q s) -> p q s", s=PACK),
-                second[:].rearrange("p (q s) -> p q s", s=PACK),
+                larger[:, :, lo // PACK : hi // PACK].rearrange("p s q -> p q s"),
+                a[t][:, lo:hi].rearrange("p (q s) -> p q s", s=PACK),
+                b[t][:, lo:hi].rearrange("p (q s) -> p q s", s=PACK),
                 ALU.max,
             )
+
+        def u_turn(larger):
             bank = turn.tile([P, PACK, P], F32, name="bank")
             for s in range(PACK):
                 nc.tensor.transpose(bank[:, s, :], larger[:, s, :], ident[:])
             return bank
 
-        def u_quantise(t, rounded):
+        def u_round(t, bank):
+            weigh_and_round(rounded[:, N + t * P : N + (t + 1) * P, :], bank, ra_sb)
+
+        def g_round(h, bank):
+            weigh_and_round(rounded[:, h * P : (h + 1) * P, :], bank, rb_sb)
+
+        def quantise(lo, hi):
             nc.vector.quantize_mx(
-                out=u_codes[t][:].bitcast(E5M2X4),
-                scales=u_scales[t][:],
-                in_=rounded.rearrange("q c s -> q (c s)"),
+                out=codes[:, lo:hi].bitcast(E5M2X4),
+                scales=scales[:, lo:hi],
+                in_=rounded[:, lo:hi, :].rearrange("q c s -> q (c s)"),
             )
 
-        def g_turn(h, picked):
+        def g_turn(h):
+            picked = g[h]
             set_sum = keep.tile([P, C], F32, name="set_sum%d" % h)
             nc.vector.tensor_reduce(
                 set_sum[:], picked[:].rearrange("p (c i) -> p c i", i=SET), mybir.AxisListType.X, ALU.add
             )
             neg_mean = keep.tile([P, C, 2], F32, name="neg_mean%d" % h)
-            nc.vector.tensor_scalar(
-                neg_mean[:], set_sum[:].unsqueeze(2).to_broadcast([P, C, 2]), -1.0 / SET, None, ALU.mult
+            nc.gpsimd.tensor_scalar(
+                neg_mean[:], set_sum[:].unsqueeze(2).to_broadcast([P, C, 2]), -1.0 / SET, 0.0, ALU.mult, ALU.add
             )
             bank = turn.tile([P, PACK, P], F32, name="bank")
             for s in range(PACK):
@@ -130,68 +147,89 @@ def tile_list_moment_larger_centred_preconditioned_pl_kernel(
                 )
             return bank
 
-        def weigh(t):
+        def moment(t):
             acc = sums.tile([P, N], F32, name="acc")
+            cols = slice(N + t * P, N + (t + 1) * P)
             nc.tensor.matmul_mx(
                 out=acc[:],
-                lhsT=u_codes[t][:].bitcast(E5M2X4),
-                lhsT_scale=u_scales[t][:],
-                rhs=g_codes[:].bitcast(E5M2X4),
-                rhs_scale=g_scales[:],
+                lhsT=codes[:, cols].bitcast(E5M2X4),
+                lhsT_scale=scales[:, cols],
+                rhs=codes[:, 0:N].bitcast(E5M2X4),
+                rhs_scale=scales[:, 0:N],
                 start=True,
                 stop=True,
             )
-            nc.vector.scalar_tensor_tensor(
-                w2[:, t, :], acc[:], 1.0, pc_sb[:, t, :], ALU.mult, ALU.mult, accum_out=row_sum[t][:]
-            )
-            nc.scalar.activation(shift[t][:], row_sum[t][:], COPY, scale=0.2 / N)
+            return acc
 
-        def update(t):
+        def weigh_v(t):
+            acc = moment(t)
+            total = keep.tile([P, 1], F32, name="total%d" % t)
+            nc.vector.scalar_tensor_tensor(
+                w2[:, t, :], acc[:], 1.0, pc_sb[:, t, :], ALU.mult, ALU.mult, accum_out=total[:]
+            )
+            nc.scalar.activation(shift[t][:], total[:], COPY, scale=0.2 / N)
+
+        def weigh_s(t):
+            acc = moment(t)
+            nc.vector.tensor_tensor(w2[:, t, :], acc[:], pc_sb[:, t, :], ALU.mult)
+            nc.scalar.activation(moved[:, t, :], w2[:, t, :], COPY, scale=0.2 / N, accum_out=shift[t][:])
+
+        def update_v(t):
             nc.vector.scalar_tensor_tensor(
                 y[:, t, :], old_sb[:, t, :], shift[t][:], w2[:, t, :], ALU.add, ALU.subtract
             )
             nc.sync.dma_start(out_rows[:, t, :], y[:, t, :])
 
-        u_bf = [keep.tile([P, P, PACK], BF16, name="u_bf%d" % t, align_bytes=64) for t in range(PACK)]
-        g_bf = keep.tile([P, N, PACK], BF16, name="g_bf", align_bytes=64)
+        def update_g(t):
+            nc.scalar.activation(moved[:, t, :], old_sb[:, t, :], IDENTITY, bias=shift[t][:])
+            nc.gpsimd.tensor_tensor(y[:, t, :], moved[:, t, :], w2[:, t, :], ALU.subtract)
+            nc.sync.dma_start(out_rows[:, t, :], y[:, t, :])
 
-        a0 = gather("vector", "a0", x_win[0], list1)
-        b0 = gather("scalar", "b0", x_win[0], list2)
-        u0 = u_turn(0, a0, b0)
-        a1 = gather("vector", "a1", x_win[1], list1)
-        b1 = gather("scalar", "b1", x_win[1], list2)
-        u1 = u_turn(1, a1, b1)
-        g0 = gather("scalar", "g0", g_win[0], list3)
-        g1 = gather("scalar", "g1", g_win[1], list3)
-        a2 = gather("scalar", "a2", x_win[2], list1)
-        b2 = gather("scalar", "b2", x_win[2], list2)
-        a3 = gather("scalar", "a3", x_win[3], list1)
-        b3 = gather("scalar", "b3", x_win[3], list2)
-        weigh_and_round(u_bf[0][:], u0, ra_sb)
-        v0 = g_turn(0, g0)
-        weigh_and_round(u_bf[1][:], u1, ra_sb)
-        v1 = g_turn(1, g1)
-        u_quantise(0, u_bf[0][:])
-        u_quantise(1, u_bf[1][:])
-        weigh_and_round(g_bf[:, 0:P, :], v0, rb_sb)
-        u2 = u_turn(2, a2, b2)
-        weigh_and_round(g_bf[:, P:N, :], v1, rb_sb)
-        weigh_and_round(u_bf[2][:], u2, ra_sb)
-        nc.vector.quantize_mx(
-            out=g_codes[:].bitcast(E5M2X4), scales=g_scales[:], in_=g_bf[:].rearrange("q c s -> q (c s)")
-        )
-        u_quantise(2, u_bf[2][:])
-        u3 = u_turn(3, a3, b3)
-        weigh(0)
-        weigh(1)
-        weigh_and_round(u_bf[3][:], u3, ra_sb)
-        update(0)
-        u_quantise(3, u_bf[3][:])
-        weigh(2)
-        update(1)
-        weigh(3)
-        update(2)
-        update(3)
+        gather("vector", a[0], x_win[0], list1, 0, J)
+        gather("scalar", b[0], x_win[0], list2, 0, J)
+        gather("vector", g[0], g_win[0], list3, 0, 128)
+        gather("scalar", g[0], g_win[0], list3, 128, J)
+        gather("scalar", g[1], g_win[1], list3, 0, J)
+        larger0 = larger_tile(0, "larger0")
+        take_larger(0, larger0, 0, J)
+        u0 = u_turn(larger0)
+        v0 = g_turn(0)
+        u_round(0, u0)
+        v1 = g_turn(1)
+        gather("vector", a[1], x_win[1], list1, 0, J)
+        gather("scalar", b[1], x_win[1], list2, 0, J)
+        gather("scalar", a[2], x_win[2], list1, 0, J)
+        gather("scalar", b[2], x_win[2], list2, 0, J)
+        gather("scalar", a[3], x_win[3], list1, 0, J // 2)
+        gather("scalar", b[3], x_win[3], list2, 0, J // 2)
+        gather("scalar", a[3], x_win[3], list1, J // 2, J)
+        gather("scalar", b[3], x_win[3], list2, J // 2, J)
+        g_round(0, v0)
+        larger1 = larger_tile(1, "larger1")
+        take_larger(1, larger1, 0, J)
+        u1 = u_turn(larger1)
+        g_round(1, v1)
+        u_round(1, u1)
+        larger2 = larger_tile(2, "larger2")
+        take_larger(2, larger2, 0, J)
+        u2 = u_turn(larger2)
+        quantise(0, N + 2 * P)
+        larger3 = larger_tile(3, "larger3")
+        take_larger(3, larger3, 0, J // 2)
+        u_round(2, u2)
+        take_larger(3, larger3, J // 2, J)
+        u3 = u_turn(larger3)
+        quantise(N + 2 * P, N + 3 * P)
+        weigh_s(0)
+        weigh_s(1)
+        u_round(3, u3)
+        weigh_s(2)
+        quantise(N + 3 * P, N + 4 * P)
+        update_v(0)
+        update_v(1)
+        weigh_v(3)
+        update_v(2)
+        update_v(3)
 
         y_bf = keep.tile([P, N, PACK], BF16, name="y_bf", align_bytes=64)
         y_woven = y[:].rearrange("p t n -> p n t")

from contextlib import ExitStack

import concourse.mybir as mybir
from concourse.masks import make_identity

K, J, N, T, V, C = 512, 512, 256, 1024, 1024, 64
FLOPS = 2 * K * J * N

F32 = mybir.dt.float32
BF16 = mybir.dt.bfloat16
I32 = mybir.dt.int32
U32 = mybir.dt.uint32
U16 = mybir.dt.uint16
U8 = mybir.dt.uint8
E5M2X4 = mybir.dt.float8_e5m2_x4
E4M3X4 = mybir.dt.float8_e4m3fn_x4
ALU = mybir.AluOpType
COPY = mybir.ActivationFunctionType.Copy
IDENTITY = mybir.ActivationFunctionType.Identity

P = 128
PACK = 4
SET = J // C
CAST_SPLIT = 176


def tile_list_moment_larger_centred_preconditioned_pl_kernel(
    tc, xf, ra, gt, rb, pc1, old, offs, offs2, offs3, out_0, out_1, out_2
):
    nc = tc.nc
    with ExitStack() as ctx:
        keep = ctx.enter_context(tc.tile_pool(name="keep", bufs=1))
        turn = ctx.enter_context(tc.psum_pool(name="turn", bufs=4))
        sums = ctx.enter_context(tc.psum_pool(name="sums", bufs=4))

        list1 = keep.tile([P, J // 16], U16, name="list1")
        list2 = keep.tile([P, J // 16], U16, name="list2")
        list3 = keep.tile([P, J // 16], U16, name="list3")
        x_win = [keep.tile([P, T], F32, name="x_win%d" % t) for t in range(PACK)]
        g_win = [keep.tile([P, V], F32, name="g_win%d" % h) for h in range(2)]
        ra_sb = keep.tile([P, PACK], F32, name="ra_sb")
        rb_sb = keep.tile([P, PACK], F32, name="rb_sb")
        pc_sb = keep.tile([P, PACK, N], F32, name="pc_sb")
        old_sb = keep.tile([P, PACK, N], F32, name="old_sb")
        ident = keep.tile([P, P], F32, name="ident")

        xf_rows = xf.rearrange("(p t) c -> p t c", t=PACK)
        nc.sync.dma_start(x_win[0][:], xf_rows[:, 0, :])
        nc.sync.dma_start(list2[:], offs2)
        nc.sync.dma_start(list1[:], offs)
        nc.sync.dma_start(list3[:], offs3)
        nc.sync.dma_start(g_win[0][:], gt[0:P, :])
        nc.sync.dma_start(g_win[1][:], gt[P : 2 * P, :])
        nc.sync.dma_start(ra_sb[:], ra.rearrange("o (p s) -> p (o s)", s=PACK))
        nc.sync.dma_start(x_win[1][:], xf_rows[:, 1, :])
        nc.sync.dma_start(rb_sb[:], rb.rearrange("o (p s) -> p (o s)", s=PACK))
        nc.sync.dma_start(x_win[2][:], xf_rows[:, 2, :])
        nc.sync.dma_start(x_win[3][:], xf_rows[:, 3, :])
        nc.sync.dma_start(pc_sb[:], pc1.rearrange("(p t) n -> p t n", t=PACK))
        nc.sync.dma_start(old_sb[:], old.rearrange("(p t) n -> p t n", t=PACK))
        make_identity(nc, ident[:])
        warm_in = keep.tile([P, 1], F32, name="warm_in")
        warm_out = keep.tile([P, 1], F32, name="warm_out")
        nc.vector.memset(warm_in[:], 0.0)
        nc.scalar.activation(warm_out[:], warm_in[:], COPY)

        def gather(engine, picked, window, offsets, lo, hi):
            source = window[:].indirect(offsets[:, lo // 16 : hi // 16])
            if engine == "vector":
                nc.vector.tensor_copy(picked[:, lo:hi], source)
            else:
                nc.scalar.activation(picked[:, lo:hi], source, COPY)

        def weigh_and_round(target, bank, weight):
            nc.vector.tensor_tensor(
                target,
                bank[:].rearrange("q s c -> q c s"),
                weight[:].unsqueeze(1).to_broadcast([P, P, PACK]),
                ALU.mult,
            )

        a = [keep.tile([P, J], F32, name="a%d" % t) for t in range(PACK)]
        b = [keep.tile([P, J], F32, name="b%d" % t) for t in range(PACK)]
        g = [keep.tile([P, J], F32, name="g%d" % h) for h in range(2)]
        codes = keep.tile([P, N + K], U32, name="codes", align_bytes=64)
        scales = keep.tile([P, N + K], U8, name="scales", align_bytes=64)
        rounded = keep.tile([P, N + K, PACK], BF16, name="rounded", align_bytes=64)
        w2 = keep.tile([P, PACK, N], F32, name="w2")
        y = keep.tile([P, PACK, N], F32, name="y")
        moved = keep.tile([P, PACK, N], F32, name="moved")
        shift = [keep.tile([P, 1], F32, name="shift%d" % t) for t in range(PACK)]
        out_rows = out_0.rearrange("(p t) n -> p t n", t=PACK)

        def larger_tile(t, tag):
            return keep.tile([P, PACK, P], F32, name="larger%d" % t, tag=tag, align_bytes=64)

        def take_larger(t, larger, lo, hi):
            nc.vector.tensor_tensor(
                larger[:, :, lo // PACK : hi // PACK].rearrange("p s q -> p q s"),
                a[t][:, lo:hi].rearrange("p (q s) -> p q s", s=PACK),
                b[t][:, lo:hi].rearrange("p (q s) -> p q s", s=PACK),
                ALU.max,
            )

        def u_turn(larger):
            bank = turn.tile([P, PACK, P], F32, name="bank")
            for s in range(PACK):
                nc.tensor.transpose(bank[:, s, :], larger[:, s, :], ident[:])
            return bank

        def u_round(t, bank):
            weigh_and_round(rounded[:, N + t * P : N + (t + 1) * P, :], bank, ra_sb)

        def g_round(h, bank):
            weigh_and_round(rounded[:, h * P : (h + 1) * P, :], bank, rb_sb)

        def quantise(lo, hi):
            nc.vector.quantize_mx(
                out=codes[:, lo:hi].bitcast(E5M2X4),
                scales=scales[:, lo:hi],
                in_=rounded[:, lo:hi, :].rearrange("q c s -> q (c s)"),
            )

        def g_turn(h):
            picked = g[h]
            set_sum = keep.tile([P, C], F32, name="set_sum%d" % h)
            nc.vector.tensor_reduce(
                set_sum[:], picked[:].rearrange("p (c i) -> p c i", i=SET), mybir.AxisListType.X, ALU.add
            )
            neg_mean = keep.tile([P, C, 2], F32, name="neg_mean%d" % h)
            nc.gpsimd.tensor_scalar(
                neg_mean[:], set_sum[:].unsqueeze(2).to_broadcast([P, C, 2]), -1.0 / SET, 0.0, ALU.mult, ALU.add
            )
            bank = turn.tile([P, PACK, P], F32, name="bank")
            for s in range(PACK):
                nc.tensor.matmul(
                    bank[:, s, :], picked[:, s:J:PACK], ident[:], start=(s == 0), stop=False, is_transpose=True
                )
            for s in range(PACK):
                nc.tensor.matmul(
                    bank[:, s, :],
                    neg_mean[:].rearrange("p c e -> p (c e)"),
                    ident[:],
                    start=False,
                    stop=(s == PACK - 1),
                    is_transpose=True,
                )
            return bank

        def moment(t):
            acc = sums.tile([P, N], F32, name="acc")
            cols = slice(N + t * P, N + (t + 1) * P)
            nc.tensor.matmul_mx(
                out=acc[:],
                lhsT=codes[:, cols].bitcast(E5M2X4),
                lhsT_scale=scales[:, cols],
                rhs=codes[:, 0:N].bitcast(E5M2X4),
                rhs_scale=scales[:, 0:N],
                start=True,
                stop=True,
            )
            return acc

        def weigh_v(t):
            acc = moment(t)
            total = keep.tile([P, 1], F32, name="total%d" % t)
            nc.vector.scalar_tensor_tensor(
                w2[:, t, :], acc[:], 1.0, pc_sb[:, t, :], ALU.mult, ALU.mult, accum_out=total[:]
            )
            nc.scalar.activation(shift[t][:], total[:], COPY, scale=0.2 / N)

        def weigh_s(t):
            acc = moment(t)
            nc.vector.tensor_tensor(w2[:, t, :], acc[:], pc_sb[:, t, :], ALU.mult)
            nc.scalar.activation(moved[:, t, :], w2[:, t, :], COPY, scale=0.2 / N, accum_out=shift[t][:])

        def update_v(t):
            nc.vector.scalar_tensor_tensor(
                y[:, t, :], old_sb[:, t, :], shift[t][:], w2[:, t, :], ALU.add, ALU.subtract
            )
            nc.sync.dma_start(out_rows[:, t, :], y[:, t, :])

        def update_g(t):
            nc.scalar.activation(moved[:, t, :], old_sb[:, t, :], IDENTITY, bias=shift[t][:])
            nc.gpsimd.tensor_tensor(y[:, t, :], moved[:, t, :], w2[:, t, :], ALU.subtract)
            nc.sync.dma_start(out_rows[:, t, :], y[:, t, :])

        gather("vector", a[0], x_win[0], list1, 0, J)
        gather("scalar", b[0], x_win[0], list2, 0, J)
        gather("vector", g[0], g_win[0], list3, 0, 128)
        gather("scalar", g[0], g_win[0], list3, 128, J)
        gather("scalar", g[1], g_win[1], list3, 0, J)
        larger0 = larger_tile(0, "larger0")
        take_larger(0, larger0, 0, J)
        u0 = u_turn(larger0)
        v0 = g_turn(0)
        u_round(0, u0)
        v1 = g_turn(1)
        gather("vector", a[1], x_win[1], list1, 0, J)
        gather("scalar", b[1], x_win[1], list2, 0, J)
        gather("scalar", a[2], x_win[2], list1, 0, J)
        gather("scalar", b[2], x_win[2], list2, 0, J)
        gather("scalar", a[3], x_win[3], list1, 0, J // 2)
        gather("scalar", b[3], x_win[3], list2, 0, J // 2)
        gather("scalar", a[3], x_win[3], list1, J // 2, J)
        gather("scalar", b[3], x_win[3], list2, J // 2, J)
        g_round(0, v0)
        larger1 = larger_tile(1, "larger1")
        take_larger(1, larger1, 0, J)
        u1 = u_turn(larger1)
        g_round(1, v1)
        u_round(1, u1)
        larger2 = larger_tile(2, "larger2")
        take_larger(2, larger2, 0, J)
        u2 = u_turn(larger2)
        quantise(0, N + 2 * P)
        larger3 = larger_tile(3, "larger3")
        take_larger(3, larger3, 0, J // 2)
        u_round(2, u2)
        take_larger(3, larger3, J // 2, J)
        u3 = u_turn(larger3)
        quantise(N + 2 * P, N + 3 * P)
        weigh_s(0)
        weigh_s(1)
        u_round(3, u3)
        weigh_s(2)
        quantise(N + 3 * P, N + 4 * P)
        update_v(0)
        update_v(1)
        weigh_v(3)
        update_v(2)
        update_v(3)

        y_bf = keep.tile([P, N, PACK], BF16, name="y_bf", align_bytes=64)
        y_woven = y[:].rearrange("p t n -> p n t")
        nc.vector.tensor_copy(y_bf[:, :CAST_SPLIT, :], y_woven[:, :CAST_SPLIT, :])
        nc.scalar.copy(y_bf[:, CAST_SPLIT:, :], y_woven[:, CAST_SPLIT:, :])
        y_codes = keep.tile([P, N], U32, name="y_codes", align_bytes=64)
        y_scales = keep.tile([P, N], U8, name="y_scales", align_bytes=64)
        nc.vector.quantize_mx(
            out=y_codes[:].bitcast(E4M3X4), scales=y_scales[:], in_=y_bf[:].rearrange("p n t -> p (n t)")
        )
        nc.sync.dma_start(out_1[0].rearrange("p c r -> p (c r)").bitcast(I32), y_codes[:].bitcast(I32))
        for quad in range(4):
            queue = nc.scalar if quad % 2 == 0 else nc.sync
            queue.dma_start(
                out_2[0, 4 * quad : 4 * quad + 4, :].bitcast(I32),
                y_scales[32 * quad : 32 * quad + 4, :].bitcast(I32),
            )
